import numpy as np
import ml_dtypes


def mxq(x, axis, fmt="e4m3"):
    dtype, down = {"e4m3": (ml_dtypes.float8_e4m3fn, 7), "e5m2": (ml_dtypes.float8_e5m2, 14)}[fmt]
    v = np.moveaxis(np.asarray(x, np.float32).astype(ml_dtypes.bfloat16).astype(np.float64), axis, -1)
    blocks = v.reshape(v.shape[:-1] + (-1, 32))
    amax = np.abs(blocks).max(-1, keepdims=True)
    byte = np.maximum(np.where(amax > 0, np.frexp(amax)[1] - 1 + 127, 0) - down, 1)
    scale = np.exp2(byte - 127.0)
    codes = (blocks / scale).astype(np.float32).astype(dtype).astype(np.float64)
    return np.moveaxis((codes * scale).reshape(v.shape), -1, axis)


WIDE = False


def mx_kscale(k):
    if not WIDE:
        return np.ones(k)
    levels = np.array([10, -10, 5, -5, 0])
    if k % 512:
        return np.exp2(np.random.permutation(np.resize(levels, k // 32))).repeat(32)
    a = np.empty((k // 512, 16))
    for p in range(k // 512):
        a[p, :8] = np.random.permutation(np.resize(levels, 8))
        for g in range(8):
            far = levels[np.abs(levels - a[p, g]) >= 10]
            a[p, g + 8] = far[np.random.randint(len(far))]
    return np.exp2(a.ravel()).repeat(32)


def f64(x):
    return np.asarray(x).astype(np.float64)


def striped(idx):
    return np.tile(idx.reshape(-1, 16).T, (8, 1)).astype(np.uint16)


def unstriped(offs):
    return offs[:16].T.reshape(-1).astype(np.int64)


def pack_weight(w):
    k, n = w.shape
    w = f64(np.asarray(w, np.float32).astype(ml_dtypes.bfloat16)).reshape(k // 32, 32, n)
    amax = np.abs(w).max(1)
    byte = np.clip(np.where(amax > 0, np.frexp(amax)[1] - 1 + 127 - 7, 1), 1, 254)
    scaled = (w * np.exp2(127.0 - byte)[:, None, :]).reshape(k, n).astype(np.float32)
    words = np.ascontiguousarray(scaled.reshape(k // 512, 128, 4, n).transpose(0, 1, 3, 2)).astype(ml_dtypes.float8_e4m3fn).view(np.uint8)
    return words, np.ascontiguousarray(byte.astype(np.uint8).reshape(k // 512, 16, n))


def unpack_weight(words, scales):
    g, p, n, _ = words.shape
    vals = np.ascontiguousarray(words).view(ml_dtypes.float8_e4m3fn).astype(np.float64) * np.repeat(np.exp2(scales.astype(np.float64) - 127.0), 8, axis=1)[..., None]
    return vals.transpose(0, 1, 3, 2).reshape(g * 512, n)


K, T, S, N, H, W, U = 512, 1024, 512, 256, 512, 1024, 1024


def setup_inputs():
    n = np.random.standard_normal
    s = mx_kscale(K)[:, None]
    u = mx_kscale(H)
    packed_xT = pack_weight(n((K, T)) * s)
    packed_eT = pack_weight(n((K, W)) * s)
    return {
        "x_words": packed_xT[0],
        "x_scales": packed_xT[1],
        "w1": (n((K, H)) / np.sqrt(K) / s).astype(np.float32),
        "w2": (n((K, H)) / np.sqrt(K) / s).astype(np.float32),
        "e_words": packed_eT[0],
        "e_scales": packed_eT[1],
        "w3": (n((K, H)) / np.sqrt(K) / s).astype(np.float32),
        "unit": (np.random.uniform(0.6, 1.4, (H, 1)) * u[:, None]).astype(np.float32),
        "w4": (n((H, N)) / np.sqrt(H) / u[:, None]).astype(np.float32),
        "offs": striped(np.random.permutation(T)[:S]),
        "sup": striped(np.random.permutation(W)[:S]),
        "itm": striped(np.random.permutation(np.concatenate([np.arange(S), np.random.randint(0, S, U - S)]))),
        "sp": striped(np.random.permutation(np.concatenate([np.arange(S), np.random.randint(0, S, U - S)]))),
    }


def reference(x_words, x_scales, w1, w2, e_words, e_scales, w3, unit, w4, offs, sup, itm, sp):
    xq = unpack_weight(x_words, x_scales)[:, unstriped(offs)]
    y = mxq(f64(w1), 0, "e4m3").T @ xq
    yi2 = y[:, unstriped(itm)]
    e_sup = unpack_weight(e_words, e_scales)[:, unstriped(sup)]
    ye = mxq(f64(w3), 0, "e4m3").T @ e_sup
    es = ye[:, unstriped(sp)]
    avl = yi2 + es
    z1 = mxq(f64(w2), 0, "e4m3").T @ xq
    zi2 = z1[:, unstriped(itm)]
    hid = f64(unit) * (np.minimum(avl, zi2) + es)
    return mxq(f64(w4), 0, "e4m3").T @ mxq(hid, 0, "e4m3")

@@ -1,0 +1,197 @@
+from contextlib import ExitStack
+
+import concourse.mybir as mybir
+
+F32 = mybir.dt.float32
+BF16 = mybir.dt.bfloat16
+I32 = mybir.dt.int32
+U32 = mybir.dt.uint32
+U16 = mybir.dt.uint16
+U8 = mybir.dt.uint8
+FP8X4 = mybir.dt.float8_e4m3fn_x4
+ALU = mybir.AluOpType
+COPY = mybir.ActivationFunctionType.Copy
+
+P = 128
+PACK = 4
+STORE = 1024
+PICKED = 512
+HIDDEN = 512
+ORDERS = 1024
+OUTS = 256
+STRIPE = 16
+SPARE = 16
+CHUNKS = (512, 256, 256)
+FLOPS = 3 * 2 * 512 * HIDDEN * PICKED + 2 * HIDDEN * OUTS * ORDERS
+
+
+def tile_picked_yinvent_cap_p_kernel(
+    tc, x_words, x_scales, w1, w2, e_words, e_scales, w3, unit, w4, offs, sup, itm, sp, out
+):
+    nc = tc.nc
+    with ExitStack() as ctx:
+        keep = ctx.enter_context(tc.tile_pool(name="keep", bufs=1))
+        psum = ctx.enter_context(tc.psum_pool(name="psum", bufs=1))
+
+        def load_list(name, src):
+            tile = keep.tile(list(src.shape), U16, name=name)
+            nc.sync.dma_start(tile[:], src)
+            return tile
+
+        def load_scales(name, src, queue):
+            tile = keep.tile([P, STORE], U8, name=name, align_bytes=64)
+            nc.gpsimd.memset(tile[:].bitcast(I32), 0)
+            for q in range(4):
+                queue.dma_start(tile[32 * q : 32 * q + 4, :].bitcast(I32), src[0, 4 * q : 4 * q + 4, :].bitcast(I32))
+            return tile
+
+        def load_words(name, src):
+            tile = keep.tile([P, STORE], U32, name=name, align_bytes=64)
+            nc.sync.dma_start(tile[:].bitcast(I32), src[0].rearrange("p n t -> p (n t)").bitcast(I32))
+            return tile
+
+        def load_halves(name, w):
+            halves = []
+            rows = w.rearrange("(p j) c -> p j c", j=PACK)
+            for h in range(2):
+                tile = keep.tile([P, PACK, HIDDEN // 2], F32, name=name + "_raw%d" % h)
+                nc.sync.dma_start(tile[:], rows[:, :, h * (HIDDEN // 2) : (h + 1) * (HIDDEN // 2)])
+                halves.append(tile)
+            return halves
+
+        def pick(name, table, offsets, dtype):
+            tile = keep.tile([P, PICKED], dtype, name=name, align_bytes=64)
+            nc.vector.tensor_copy(tile[:], table[:].indirect(offsets[:]))
+            return tile
+
+        def quantise_dealt(name, halves, copies):
+            grouped = keep.tile([P, PACK, P, PACK], BF16, name=name + "_bf", align_bytes=64)
+            for h in range(2):
+                copies[h](
+                    grouped[:, :, h * (P // 2) : (h + 1) * (P // 2), :].rearrange("p t m j -> p m j t"),
+                    halves[h][:].rearrange("p j (m t) -> p m j t", t=PACK),
+                )
+            codes = keep.tile([P, HIDDEN], U32, name=name + "_codes", align_bytes=64)
+            scales = keep.tile([P, HIDDEN], U8, name=name + "_scales", align_bytes=64)
+            for t in range(PACK):
+                nc.vector.quantize_mx(
+                    out=codes[:, t * P : (t + 1) * P].bitcast(FP8X4),
+                    scales=scales[:, t * P : (t + 1) * P],
+                    in_=grouped[:, t, :, :].rearrange("p m j -> p (m j)"),
+                )
+            return codes, scales
+
+        def on_scalar(dst, src, factor):
+            nc.scalar.activation(dst, src, COPY, scale=factor)
+
+        def on_vector(dst, src, factor):
+            nc.vector.tensor_scalar(dst, src, factor, None, ALU.mult)
+
+        def project(name, weight, words, scale_bytes, size, empty):
+            codes, scales = weight
+            windows = []
+            for t in range(PACK):
+                acc = psum.tile([P, PICKED], F32, name="acc", bufs=6)
+                nc.tensor.matmul_mx(
+                    out=acc[:],
+                    lhsT=codes[:, t * P : (t + 1) * P].bitcast(FP8X4),
+                    lhsT_scale=scales[:, t * P : (t + 1) * P],
+                    rhs=words[:].bitcast(FP8X4),
+                    rhs_scale=scale_bytes[:],
+                    start=True,
+                    stop=True,
+                )
+                window = keep.tile([P, PICKED + SPARE], F32, name=name + "%d" % t)
+                nc.gpsimd.memset(window[:, PICKED:], 0.0)
+                empty(window[:, :PICKED], acc[:], size[:, t : t + 1])
+                windows.append(window)
+            return windows
+
+        sup_t = load_list("sup_t", sup)
+        unit_t = keep.tile([P, PACK], F32, name="unit_t")
+        nc.sync.dma_start(unit_t[:], unit.rearrange("(p t) o -> p (t o)", t=PACK))
+        e_word_table = load_words("e_word_table", e_words)
+        e_scale_table = load_scales("e_scale_table", e_scales, nc.sync)
+        w3_raw = load_halves("w3", w3)
+        offs_t = load_list("offs_t", offs)
+        x_word_table = load_words("x_word_table", x_words)
+        x_scale_table = load_scales("x_scale_table", x_scales, nc.sync)
+        w1_raw = load_halves("w1", w1)
+        sp_t = load_list("sp_t", sp)
+        itm_t = load_list("itm_t", itm)
+        w2_raw = load_halves("w2", w2)
+        w4_raw = keep.tile([P, PACK, OUTS], F32, name="w4_raw")
+        nc.sync.dma_start(w4_raw[:], w4.rearrange("(p j) c -> p j c", j=PACK))
+
+        twice = keep.tile([P, PACK], F32, name="twice")
+        sign = keep.tile([P, PACK], F32, name="sign")
+        size = keep.tile([P, PACK], F32, name="size")
+        nc.gpsimd.tensor_scalar(twice[:], unit_t[:], 0.0, 2.0, ALU.is_ge, ALU.mult)
+        nc.gpsimd.tensor_scalar(sign[:], twice[:], 1.0, -1.0, ALU.mult, ALU.add)
+        nc.gpsimd.tensor_tensor(size[:], unit_t[:], sign[:], ALU.mult)
+
+        e_picked = pick("e_picked", e_word_table, sup_t, U32)
+        e_bytes = pick("e_bytes", e_scale_table, sup_t, U8)
+        w3_q = quantise_dealt("w3", w3_raw, (nc.scalar.copy, nc.vector.tensor_copy))
+        ye = project("ye", w3_q, e_picked, e_bytes, size, on_scalar)
+        x_picked = pick("x_picked", x_word_table, offs_t, U32)
+        x_bytes = pick("x_bytes", x_scale_table, offs_t, U8)
+        w1_q = quantise_dealt("w1", w1_raw, (nc.vector.tensor_copy, nc.vector.tensor_copy))
+        y = project("y", w1_q, x_picked, x_bytes, size, on_vector)
+        w2_q = quantise_dealt("w2", w2_raw, (nc.vector.tensor_copy, nc.vector.tensor_copy))
+        z = project("z", w2_q, x_picked, x_bytes, size, on_scalar)
+
+        w4_bf = keep.tile([P, OUTS, PACK], BF16, name="w4_bf", align_bytes=64)
+        nc.vector.tensor_tensor(
+            w4_bf[:].rearrange("p (c i) j -> p c j i", i=4),
+            w4_raw[:].rearrange("p j (c i) -> p c j i", i=4),
+            sign[:].unsqueeze(1).unsqueeze(3).to_broadcast([P, OUTS // 4, PACK, 4]),
+            ALU.mult,
+        )
+        w4_codes = keep.tile([P, OUTS], U32, name="w4_codes", align_bytes=64)
+        w4_scales = keep.tile([P, OUTS], U8, name="w4_scales", align_bytes=64)
+        nc.vector.quantize_mx(
+            out=w4_codes[:].bitcast(FP8X4), scales=w4_scales[:], in_=w4_bf[:].rearrange("p c j -> p (c j)")
+        )
+
+        out_rows = out.rearrange("(m p) r -> p m r", p=P)
+        first = 0
+        for c, n in enumerate(CHUNKS):
+            entries = slice(first // STRIPE, (first + n) // STRIPE)
+            es = keep.tile([P, PACK, n], F32, name="es%d" % c)
+            zi = keep.tile([P, PACK, n], F32, name="zi%d" % c)
+            avl = keep.tile([P, PACK, n], F32, name="avl%d" % c)
+            for t in range(PACK):
+                nc.scalar.activation(es[:, t, :], ye[t][:].indirect(sp_t[:, entries]), COPY)
+            for t in range(PACK):
+                nc.vector.tensor_tensor(avl[:, t, :], y[t][:].indirect(itm_t[:, entries]), es[:, t, :], ALU.add)
+                nc.scalar.activation(zi[:, t, :], z[t][:].indirect(itm_t[:, entries]), COPY)
+            for t in range(0, PACK, 2):
+                nc.vector.tensor_tensor(avl[:, t : t + 2, :], avl[:, t : t + 2, :], zi[:, t : t + 2, :], ALU.min)
+            hid = keep.tile([P, n, PACK], BF16, name="hid%d" % c, align_bytes=64)
+            nc.vector.tensor_tensor(
+                hid[:].rearrange("p (c i) t -> p c t i", i=4),
+                avl[:].rearrange("p t (c i) -> p c t i", i=4),
+                es[:].rearrange("p t (c i) -> p c t i", i=4),
+                ALU.add,
+            )
+            hid_codes = keep.tile([P, n], U32, name="hid_codes%d" % c, align_bytes=64)
+            hid_scales = keep.tile([P, n], U8, name="hid_scales%d" % c, align_bytes=64)
+            nc.vector.quantize_mx(
+                out=hid_codes[:].bitcast(FP8X4), scales=hid_scales[:], in_=hid[:].rearrange("p c t -> p (c t)")
+            )
+            result = keep.tile([P, OUTS // P, n], F32, name="result%d" % c)
+            for m in range(OUTS // P):
+                acc = psum.tile([P, n], F32, name="out_acc", bufs=2)
+                nc.tensor.matmul_mx(
+                    out=acc[:],
+                    lhsT=w4_codes[:, m * P : (m + 1) * P].bitcast(FP8X4),
+                    lhsT_scale=w4_scales[:, m * P : (m + 1) * P],
+                    rhs=hid_codes[:].bitcast(FP8X4),
+                    rhs_scale=hid_scales[:],
+                    start=True,
+                    stop=True,
+                )
+                nc.scalar.copy(result[:, m, :], acc[:])
+                nc.sync.dma_start(out_rows[:, m, first : first + n], result[:, m, :])
+            first += n

@@ -21,7 +21,8 @@ ORDERS = 1024
 OUTS = 256
 STRIPE = 16
 SPARE = 16
-CHUNKS = (512, 256, 256)
+HALF = ORDERS // 2
+CHUNKS = (256, 256, 256, 128, 128)
 FLOPS = 3 * 2 * 512 * HIDDEN * PICKED + 2 * HIDDEN * OUTS * ORDERS
 
 
@@ -68,8 +69,8 @@ def tile_picked_yinvent_cap_p_kernel(
             grouped = keep.tile([P, PACK, P, PACK], BF16, name=name + "_bf", align_bytes=64)
             for h in range(2):
                 copies[h](
-                    grouped[:, :, h * (P // 2) : (h + 1) * (P // 2), :].rearrange("p t m j -> p m j t"),
-                    halves[h][:].rearrange("p j (m t) -> p m j t", t=PACK),
+                    grouped[:, :, h * (P // 2) : (h + 1) * (P // 2), :].rearrange("p t m j -> p m t j"),
+                    halves[h][:].rearrange("p j (m t) -> p m t j", t=PACK),
                 )
             codes = keep.tile([P, HIDDEN], U32, name=name + "_codes", align_bytes=64)
             scales = keep.tile([P, HIDDEN], U8, name=name + "_scales", align_bytes=64)
@@ -81,6 +82,9 @@ def tile_picked_yinvent_cap_p_kernel(
                 )
             return codes, scales
 
+        def round_on_gpsimd(dst, src):
+            nc.gpsimd.tensor_scalar(dst, src, 1.0, 0.0, ALU.mult, ALU.add)
+
         def on_scalar(dst, src, factor):
             nc.scalar.activation(dst, src, COPY, scale=factor)
 
@@ -91,7 +95,7 @@ def tile_picked_yinvent_cap_p_kernel(
             codes, scales = weight
             windows = []
             for t in range(PACK):
-                acc = psum.tile([P, PICKED], F32, name="acc", bufs=6)
+                acc = psum.tile([P, PICKED], F32, name="acc", bufs=8)
                 nc.tensor.matmul_mx(
                     out=acc[:],
                     lhsT=codes[:, t * P : (t + 1) * P].bitcast(FP8X4),
@@ -103,7 +107,7 @@ def tile_picked_yinvent_cap_p_kernel(
                 )
                 window = keep.tile([P, PICKED + SPARE], F32, name=name + "%d" % t)
                 nc.gpsimd.memset(window[:, PICKED:], 0.0)
-                empty(window[:, :PICKED], acc[:], size[:, t : t + 1])
+                empty[t % 2](window[:, :PICKED], acc[:], size[:, t : t + 1])
                 windows.append(window)
             return windows
 
@@ -116,8 +120,8 @@ def tile_picked_yinvent_cap_p_kernel(
         offs_t = load_list("offs_t", offs)
         x_word_table = load_words("x_word_table", x_words)
         x_scale_table = load_scales("x_scale_table", x_scales, nc.sync)
-        w1_raw = load_halves("w1", w1)
         sp_t = load_list("sp_t", sp)
+        w1_raw = load_halves("w1", w1)
         itm_t = load_list("itm_t", itm)
         w2_raw = load_halves("w2", w2)
         w4_raw = keep.tile([P, PACK, OUTS], F32, name="w4_raw")
@@ -133,13 +137,22 @@ def tile_picked_yinvent_cap_p_kernel(
         e_picked = pick("e_picked", e_word_table, sup_t, U32)
         e_bytes = pick("e_bytes", e_scale_table, sup_t, U8)
         w3_q = quantise_dealt("w3", w3_raw, (nc.scalar.copy, nc.vector.tensor_copy))
-        ye = project("ye", w3_q, e_picked, e_bytes, size, on_scalar)
+        ye = project("ye", w3_q, e_picked, e_bytes, size, (on_scalar, on_scalar))
         x_picked = pick("x_picked", x_word_table, offs_t, U32)
         x_bytes = pick("x_bytes", x_scale_table, offs_t, U8)
-        w1_q = quantise_dealt("w1", w1_raw, (nc.vector.tensor_copy, nc.vector.tensor_copy))
-        y = project("y", w1_q, x_picked, x_bytes, size, on_vector)
-        w2_q = quantise_dealt("w2", w2_raw, (nc.vector.tensor_copy, nc.vector.tensor_copy))
-        z = project("z", w2_q, x_picked, x_bytes, size, on_scalar)
+        w1_q = quantise_dealt("w1", w1_raw, (round_on_gpsimd, nc.vector.tensor_copy))
+        y = project("y", w1_q, x_picked, x_bytes, size, (on_vector, on_vector))
+        w2_q = quantise_dealt("w2", w2_raw, (round_on_gpsimd, round_on_gpsimd))
+        z = project("z", w2_q, x_picked, x_bytes, size, (on_scalar, on_scalar))
+
+        es, avl = [], []
+        for h in range(2):
+            entries = slice(h * HALF // STRIPE, (h + 1) * HALF // STRIPE)
+            es.append(keep.tile([P, PACK, HALF], F32, name="es%d" % h))
+            avl.append(keep.tile([P, PACK, HALF], F32, name="avl%d" % h))
+            for t in range(PACK):
+                nc.scalar.activation(es[h][:, t, :], ye[t][:].indirect(sp_t[:, entries]), COPY)
+                nc.vector.tensor_tensor(avl[h][:, t, :], y[t][:].indirect(itm_t[:, entries]), es[h][:, t, :], ALU.add)
 
         w4_bf = keep.tile([P, OUTS, PACK], BF16, name="w4_bf", align_bytes=64)
         nc.vector.tensor_tensor(
@@ -155,36 +168,38 @@ def tile_picked_yinvent_cap_p_kernel(
         )
 
         out_rows = out.rearrange("(m p) r -> p m r", p=P)
-        first = 0
-        for c, n in enumerate(CHUNKS):
+
+        def cut(first, n):
             entries = slice(first // STRIPE, (first + n) // STRIPE)
-            es = keep.tile([P, PACK, n], F32, name="es%d" % c)
-            zi = keep.tile([P, PACK, n], F32, name="zi%d" % c)
-            avl = keep.tile([P, PACK, n], F32, name="avl%d" % c)
+            h, cols = first // HALF, slice(first % HALF, first % HALF + n)
+            zi = keep.tile([P, PACK, n], F32, name="zi%d" % first)
             for t in range(PACK):
-                nc.scalar.activation(es[:, t, :], ye[t][:].indirect(sp_t[:, entries]), COPY)
-            for t in range(PACK):
-                nc.vector.tensor_tensor(avl[:, t, :], y[t][:].indirect(itm_t[:, entries]), es[:, t, :], ALU.add)
                 nc.scalar.activation(zi[:, t, :], z[t][:].indirect(itm_t[:, entries]), COPY)
             for t in range(0, PACK, 2):
-                nc.vector.tensor_tensor(avl[:, t : t + 2, :], avl[:, t : t + 2, :], zi[:, t : t + 2, :], ALU.min)
-            hid = keep.tile([P, n, PACK], BF16, name="hid%d" % c, align_bytes=64)
+                nc.vector.tensor_tensor(zi[:, t : t + 2, :], avl[h][:, t : t + 2, cols], zi[:, t : t + 2, :], ALU.min)
+            return zi
+
+        def add_supplier(first, n, capped):
+            h, cols = first // HALF, slice(first % HALF, first % HALF + n)
+            hid = keep.tile([P, n, PACK], BF16, name="hid%d" % first, align_bytes=64)
             nc.vector.tensor_tensor(
                 hid[:].rearrange("p (c i) t -> p c t i", i=4),
-                avl[:].rearrange("p t (c i) -> p c t i", i=4),
-                es[:].rearrange("p t (c i) -> p c t i", i=4),
+                capped[:].rearrange("p t (c i) -> p c t i", i=4),
+                es[h][:, :, cols].rearrange("p t (c i) -> p c t i", i=4),
                 ALU.add,
             )
-            hid_codes = keep.tile([P, n], U32, name="hid_codes%d" % c, align_bytes=64)
-            hid_scales = keep.tile([P, n], U8, name="hid_scales%d" % c, align_bytes=64)
+            return hid
+
+        def last_product(first, n, hid):
+            hid_codes = keep.tile([P, n], U32, name="hid_codes%d" % first, align_bytes=64)
+            hid_scales = keep.tile([P, n], U8, name="hid_scales%d" % first, align_bytes=64)
             nc.vector.quantize_mx(
                 out=hid_codes[:].bitcast(FP8X4), scales=hid_scales[:], in_=hid[:].rearrange("p c t -> p (c t)")
             )
-            result = keep.tile([P, OUTS // P, n], F32, name="result%d" % c)
+            acc = psum.tile([P, OUTS // P, n], F32, name="acc", bufs=8)
             for m in range(OUTS // P):
-                acc = psum.tile([P, n], F32, name="out_acc", bufs=2)
                 nc.tensor.matmul_mx(
-                    out=acc[:],
+                    out=acc[:, m, :],
                     lhsT=w4_codes[:, m * P : (m + 1) * P].bitcast(FP8X4),
                     lhsT_scale=w4_scales[:, m * P : (m + 1) * P],
                     rhs=hid_codes[:].bitcast(FP8X4),
@@ -192,6 +207,15 @@ def tile_picked_yinvent_cap_p_kernel(
                     start=True,
                     stop=True,
                 )
-                nc.scalar.copy(result[:, m, :], acc[:])
-                nc.sync.dma_start(out_rows[:, m, first : first + n], result[:, m, :])
+            result = keep.tile([P, OUTS // P, n], F32, name="result%d" % first)
+            nc.scalar.copy(result[:], acc[:])
+            nc.sync.dma_start(out_rows[:, :, first : first + n], result[:])
+
+        first, waiting = 0, None
+        for n in CHUNKS:
+            capped = cut(first, n)
+            if waiting is not None:
+                last_product(*waiting)
+            waiting = (first, n, add_supplier(first, n, capped))
             first += n
+        last_product(*waiting)

from contextlib import ExitStack

import concourse.mybir as mybir

F32 = mybir.dt.float32
BF16 = mybir.dt.bfloat16
I32 = mybir.dt.int32
U32 = mybir.dt.uint32
U16 = mybir.dt.uint16
U8 = mybir.dt.uint8
FP8X4 = mybir.dt.float8_e4m3fn_x4
ALU = mybir.AluOpType
COPY = mybir.ActivationFunctionType.Copy

P = 128
PACK = 4
STORE = 1024
PICKED = 512
HIDDEN = 512
ORDERS = 1024
OUTS = 256
STRIPE = 16
SPARE = 16
HALF = ORDERS // 2
CHUNKS = (256, 256, 256, 128, 128)
FLOPS = 3 * 2 * 512 * HIDDEN * PICKED + 2 * HIDDEN * OUTS * ORDERS


def tile_picked_yinvent_cap_p_kernel(
    tc, x_words, x_scales, w1, w2, e_words, e_scales, w3, unit, w4, offs, sup, itm, sp, out
):
    nc = tc.nc
    with ExitStack() as ctx:
        keep = ctx.enter_context(tc.tile_pool(name="keep", bufs=1))
        psum = ctx.enter_context(tc.psum_pool(name="psum", bufs=1))

        def load_list(name, src):
            tile = keep.tile(list(src.shape), U16, name=name)
            nc.sync.dma_start(tile[:], src)
            return tile

        def load_scales(name, src, queue):
            tile = keep.tile([P, STORE], U8, name=name, align_bytes=64)
            nc.gpsimd.memset(tile[:].bitcast(I32), 0)
            for q in range(4):
                queue.dma_start(tile[32 * q : 32 * q + 4, :].bitcast(I32), src[0, 4 * q : 4 * q + 4, :].bitcast(I32))
            return tile

        def load_words(name, src):
            tile = keep.tile([P, STORE], U32, name=name, align_bytes=64)
            nc.sync.dma_start(tile[:].bitcast(I32), src[0].rearrange("p n t -> p (n t)").bitcast(I32))
            return tile

        def load_halves(name, w):
            halves = []
            rows = w.rearrange("(p j) c -> p j c", j=PACK)
            for h in range(2):
                tile = keep.tile([P, PACK, HIDDEN // 2], F32, name=name + "_raw%d" % h)
                nc.sync.dma_start(tile[:], rows[:, :, h * (HIDDEN // 2) : (h + 1) * (HIDDEN // 2)])
                halves.append(tile)
            return halves

        def pick(name, table, offsets, dtype):
            tile = keep.tile([P, PICKED], dtype, name=name, align_bytes=64)
            nc.vector.tensor_copy(tile[:], table[:].indirect(offsets[:]))
            return tile

        def quantise_dealt(name, halves, copies):
            grouped = keep.tile([P, PACK, P, PACK], BF16, name=name + "_bf", align_bytes=64)
            for h in range(2):
                copies[h](
                    grouped[:, :, h * (P // 2) : (h + 1) * (P // 2), :].rearrange("p t m j -> p m t j"),
                    halves[h][:].rearrange("p j (m t) -> p m t j", t=PACK),
                )
            codes = keep.tile([P, HIDDEN], U32, name=name + "_codes", align_bytes=64)
            scales = keep.tile([P, HIDDEN], U8, name=name + "_scales", align_bytes=64)
            for t in range(PACK):
                nc.vector.quantize_mx(
                    out=codes[:, t * P : (t + 1) * P].bitcast(FP8X4),
                    scales=scales[:, t * P : (t + 1) * P],
                    in_=grouped[:, t, :, :].rearrange("p m j -> p (m j)"),
                )
            return codes, scales

        def round_on_gpsimd(dst, src):
            nc.gpsimd.tensor_scalar(dst, src, 1.0, 0.0, ALU.mult, ALU.add)

        def on_scalar(dst, src, factor):
            nc.scalar.activation(dst, src, COPY, scale=factor)

        def on_vector(dst, src, factor):
            nc.vector.tensor_scalar(dst, src, factor, None, ALU.mult)

        def project(name, weight, words, scale_bytes, size, empty):
            codes, scales = weight
            windows = []
            for t in range(PACK):
                acc = psum.tile([P, PICKED], F32, name="acc", bufs=8)
                nc.tensor.matmul_mx(
                    out=acc[:],
                    lhsT=codes[:, t * P : (t + 1) * P].bitcast(FP8X4),
                    lhsT_scale=scales[:, t * P : (t + 1) * P],
                    rhs=words[:].bitcast(FP8X4),
                    rhs_scale=scale_bytes[:],
                    start=True,
                    stop=True,
                )
                window = keep.tile([P, PICKED + SPARE], F32, name=name + "%d" % t)
                nc.gpsimd.memset(window[:, PICKED:], 0.0)
                empty[t % 2](window[:, :PICKED], acc[:], size[:, t : t + 1])
                windows.append(window)
            return windows

        sup_t = load_list("sup_t", sup)
        unit_t = keep.tile([P, PACK], F32, name="unit_t")
        nc.sync.dma_start(unit_t[:], unit.rearrange("(p t) o -> p (t o)", t=PACK))
        e_word_table = load_words("e_word_table", e_words)
        e_scale_table = load_scales("e_scale_table", e_scales, nc.sync)
        w3_raw = load_halves("w3", w3)
        offs_t = load_list("offs_t", offs)
        x_word_table = load_words("x_word_table", x_words)
        x_scale_table = load_scales("x_scale_table", x_scales, nc.sync)
        sp_t = load_list("sp_t", sp)
        w1_raw = load_halves("w1", w1)
        itm_t = load_list("itm_t", itm)
        w2_raw = load_halves("w2", w2)
        w4_raw = keep.tile([P, PACK, OUTS], F32, name="w4_raw")
        nc.sync.dma_start(w4_raw[:], w4.rearrange("(p j) c -> p j c", j=PACK))

        twice = keep.tile([P, PACK], F32, name="twice")
        sign = keep.tile([P, PACK], F32, name="sign")
        size = keep.tile([P, PACK], F32, name="size")
        nc.gpsimd.tensor_scalar(twice[:], unit_t[:], 0.0, 2.0, ALU.is_ge, ALU.mult)
        nc.gpsimd.tensor_scalar(sign[:], twice[:], 1.0, -1.0, ALU.mult, ALU.add)
        nc.gpsimd.tensor_tensor(size[:], unit_t[:], sign[:], ALU.mult)

        e_picked = pick("e_picked", e_word_table, sup_t, U32)
        e_bytes = pick("e_bytes", e_scale_table, sup_t, U8)
        w3_q = quantise_dealt("w3", w3_raw, (nc.scalar.copy, nc.vector.tensor_copy))
        ye = project("ye", w3_q, e_picked, e_bytes, size, (on_scalar, on_scalar))
        x_picked = pick("x_picked", x_word_table, offs_t, U32)
        x_bytes = pick("x_bytes", x_scale_table, offs_t, U8)
        w1_q = quantise_dealt("w1", w1_raw, (round_on_gpsimd, nc.vector.tensor_copy))
        y = project("y", w1_q, x_picked, x_bytes, size, (on_vector, on_vector))
        w2_q = quantise_dealt("w2", w2_raw, (round_on_gpsimd, round_on_gpsimd))
        z = project("z", w2_q, x_picked, x_bytes, size, (on_scalar, on_scalar))

        es, avl = [], []
        for h in range(2):
            entries = slice(h * HALF // STRIPE, (h + 1) * HALF // STRIPE)
            es.append(keep.tile([P, PACK, HALF], F32, name="es%d" % h))
            avl.append(keep.tile([P, PACK, HALF], F32, name="avl%d" % h))
            for t in range(PACK):
                nc.scalar.activation(es[h][:, t, :], ye[t][:].indirect(sp_t[:, entries]), COPY)
                nc.vector.tensor_tensor(avl[h][:, t, :], y[t][:].indirect(itm_t[:, entries]), es[h][:, t, :], ALU.add)

        w4_bf = keep.tile([P, OUTS, PACK], BF16, name="w4_bf", align_bytes=64)
        nc.vector.tensor_tensor(
            w4_bf[:].rearrange("p (c i) j -> p c j i", i=4),
            w4_raw[:].rearrange("p j (c i) -> p c j i", i=4),
            sign[:].unsqueeze(1).unsqueeze(3).to_broadcast([P, OUTS // 4, PACK, 4]),
            ALU.mult,
        )
        w4_codes = keep.tile([P, OUTS], U32, name="w4_codes", align_bytes=64)
        w4_scales = keep.tile([P, OUTS], U8, name="w4_scales", align_bytes=64)
        nc.vector.quantize_mx(
            out=w4_codes[:].bitcast(FP8X4), scales=w4_scales[:], in_=w4_bf[:].rearrange("p c j -> p (c j)")
        )

        out_rows = out.rearrange("(m p) r -> p m r", p=P)

        def cut(first, n):
            entries = slice(first // STRIPE, (first + n) // STRIPE)
            h, cols = first // HALF, slice(first % HALF, first % HALF + n)
            zi = keep.tile([P, PACK, n], F32, name="zi%d" % first)
            for t in range(PACK):
                nc.scalar.activation(zi[:, t, :], z[t][:].indirect(itm_t[:, entries]), COPY)
            for t in range(0, PACK, 2):
                nc.vector.tensor_tensor(zi[:, t : t + 2, :], avl[h][:, t : t + 2, cols], zi[:, t : t + 2, :], ALU.min)
            return zi

        def add_supplier(first, n, capped):
            h, cols = first // HALF, slice(first % HALF, first % HALF + n)
            hid = keep.tile([P, n, PACK], BF16, name="hid%d" % first, align_bytes=64)
            nc.vector.tensor_tensor(
                hid[:].rearrange("p (c i) t -> p c t i", i=4),
                capped[:].rearrange("p t (c i) -> p c t i", i=4),
                es[h][:, :, cols].rearrange("p t (c i) -> p c t i", i=4),
                ALU.add,
            )
            return hid

        def last_product(first, n, hid):
            hid_codes = keep.tile([P, n], U32, name="hid_codes%d" % first, align_bytes=64)
            hid_scales = keep.tile([P, n], U8, name="hid_scales%d" % first, align_bytes=64)
            nc.vector.quantize_mx(
                out=hid_codes[:].bitcast(FP8X4), scales=hid_scales[:], in_=hid[:].rearrange("p c t -> p (c t)")
            )
            acc = psum.tile([P, OUTS // P, n], F32, name="acc", bufs=8)
            for m in range(OUTS // P):
                nc.tensor.matmul_mx(
                    out=acc[:, m, :],
                    lhsT=w4_codes[:, m * P : (m + 1) * P].bitcast(FP8X4),
                    lhsT_scale=w4_scales[:, m * P : (m + 1) * P],
                    rhs=hid_codes[:].bitcast(FP8X4),
                    rhs_scale=hid_scales[:],
                    start=True,
                    stop=True,
                )
            result = keep.tile([P, OUTS // P, n], F32, name="result%d" % first)
            nc.scalar.copy(result[:], acc[:])
            nc.sync.dma_start(out_rows[:, :, first : first + n], result[:])

        first, waiting = 0, None
        for n in CHUNKS:
            capped = cut(first, n)
            if waiting is not None:
                last_product(*waiting)
            waiting = (first, n, add_supplier(first, n, capped))
            first += n
        last_product(*waiting)
